import numpy as np, ml_dtypes
CORES = [29,45,93,109,157,173,221,237,285,301,349,365,413,429,477,493]
N = 16
import mx_ref
NC = 256
BF = ml_dtypes.bfloat16
def setup_inputs(rng):
    def f(*shape):
        return mx_ref.flush((rng.standard_normal(shape, dtype=np.float32) * np.exp2(rng.integers(-2, 3, shape[:-1] + (1,)))).astype(BF))
    return {"w": f(N, 128, 512), "x": f(N, 128, 4 * NC)}
def setup_inputs_blocks(rng):
    d = setup_inputs(rng)
    for k in ("w", "x"): d[k] = mx_ref.spread(d[k], rng, 4)
    return d
def setup_inputs_wide(rng):
    d = setup_inputs(rng)
    for k in ("w", "x"): d[k] = mx_ref.flush((d[k].astype(np.float32) * np.exp2(rng.integers(-8, 9, (N, 1, 1))).astype(np.float32)).astype(BF))
    return d
def reference(w, x):
    QX = [mx_ref.quantize(x[j]) for j in range(N)]
    y = np.zeros((N, 128, NC), np.float32)
    for r in range(N):
        qw = mx_ref.quantize(w[r])
        for j in range(N):
            p = mx_ref.matmul(qw, QX[j])
            y[r] = p if j == 0 else np.maximum(y[r], p)
    return {"y": y}

@@ -1,0 +1,171 @@
+from concourse.bass import DstId, RemoteDMATransfer
+from concourse.mybir import dt, AluOpType
+
+N = 16
+NC = 256
+WORLD = 512
+BANK = 512
+BANKS = 8
+
+SCRATCH = {
+    "xb": ("sbuf", [128, 4 * NC], "bfloat16"),
+    "wb": ("sbuf", [128, 512], "bfloat16"),
+    "qw": ("sbuf", [128, 128], "float8_e4m3fn_x4"),
+    "sw": ("sbuf", [128, 128], "uint8"),
+    "qx": ("sbuf", [128, N * NC], "float8_e4m3fn_x4"),
+    "sx": ("sbuf", [128, N * NC], "uint8"),
+    "acc": ("sbuf", [128, NC], "float32"),
+    "ps": ("psum", [128, BANK * BANKS], "float32"),
+}
+SEMAPHORES = (["xin", "win", "xq", "wq", "vm", "out", "sent"]
+              + ["c%d" % t for t in range(N)]
+              + ["s%d" % t for t in range(N)]
+              + ["m%d" % t for t in range(N)])
+
+_CACHE = {}
+
+
+def _bits(m):
+    return bin(m).count("1")
+
+
+def _build(T, topo):
+    ranks = list(T.cores)
+    hosts = sorted(set(topo.host(r) for r in ranks))
+    row = {}
+    for h in hosts:
+        row[h] = sorted([r for r in ranks if topo.host(r) == h], key=topo.chip)
+    helpers = {}
+    for r in ranks:
+        chip = [c for c in range(WORLD) if c != r and topo.host(c) == topo.host(r) and topo.chip(c) == topo.chip(r)]
+        other = [c for c in chip if topo.die(c) != topo.die(r)]
+        same = [c for c in chip if topo.die(c) == topo.die(r)]
+        helpers[r] = (other[1], other[0], same[-1], other[2])
+    first, relay = {}, {}
+    when = {}
+    for r in ranks:
+        when[r] = {}
+    lag = 1.5
+    for t, r in enumerate(ranks):
+        h = topo.host(r)
+        n = len(row[h])
+        i = row[h].index(r)
+        mate_host = [k for k in hosts if k != h and topo.rack(k) == topo.rack(h)][0]
+        far = [k for k in hosts if topo.rack(k) != topo.rack(h)]
+        cabled = [k for k in far if topo.may_write(r, row[k][i])][0]
+        diagonal = [k for k in far if k != cabled][0]
+
+        def at(k, s):
+            return row[k][(i + s) % n]
+
+        tree = [
+            (at(cabled, 0), [at(diagonal, s) for s in range(n)]),
+            (at(h, 1), [at(cabled, 1), at(mate_host, 1), at(mate_host, 0)]),
+            (at(h, 2), [at(cabled, 2), at(mate_host, 2)]),
+            (at(h, 3), [at(cabled, 3)]),
+        ]
+        first[r] = []
+        for j, (home, kids) in enumerate(tree):
+            q = helpers[home][j]
+            first[r].append(q)
+            relay[q] = (t, home, kids)
+            when[home][t] = j + 1 + lag + 1
+            for k, d in enumerate(kids):
+                when[d][t] = j + 1 + lag + k + 1
+        first[r].append(at(mate_host, 3))
+        when[at(mate_host, 3)][t] = len(tree) + 1
+        when[r][t] = 0
+    return first, relay, when
+
+
+def _codes(T, t):
+    return T.qx[:, t * NC:(t + 1) * NC].bitcast(dt.uint8)
+
+
+def _plane(T, t):
+    return T.sx[:, t * NC:(t + 1) * NC]
+
+
+def _helper(g, core, T, topo, job):
+    t, home, kids = job
+    away = topo.mask(core, kids[0])
+    here = topo.mask(core, home) & ~away
+    ids = []
+    for d in kids:
+        rid, pid = topo.addr(d, core)
+        ids.append(DstId(rid=rid, pnc=pid))
+    rid, pid = topo.addr(home, core)
+    home_id = DstId(rid=rid, pnc=pid)
+    sent = 0
+    for view, sem in ((_plane, T.sem["s%d" % t]), (_codes, T.sem["c%d" % t])):
+        g.wait_ge(sem, _bits(away))
+        g.remote_dma_fused([
+            RemoteDMATransfer(dst_ids=ids, dma_engine_mask=away, remote_sem=sem,
+                              srcs=[view(T, t)], dsts=[view(T, t) for d in kids]),
+            RemoteDMATransfer(dst_ids=[home_id], dma_engine_mask=here, remote_sem=sem,
+                              src=view(T, t), dst=view(T, t)),
+        ], local_sem=T.sem.sent)
+        sent += _bits(away) + _bits(here)
+    g.wait_ge(T.sem.sent, sent)
+
+
+def rank_program(g, core, T, topo):
+    if "plan" not in _CACHE:
+        _CACHE["plan"] = _build(T, topo)
+    first, relay, when = _CACHE["plan"]
+    rank = T.rank_of(core)
+    if rank is None:
+        if core in relay:
+            _helper(g, core, T, topo, relay[core])
+        return
+
+    g.sync.dma_start(T.xb[:], T.x[:]).then_inc(T.sem.xin, 16)
+    g.scalar.wait_ge(T.sem.xin, 16)
+    g.scalar.dma_start(T.wb[:], T.w[:]).then_inc(T.sem.win, 16)
+
+    own = slice(rank * NC, (rank + 1) * NC)
+    g.vector.wait_ge(T.sem.xin, 16)
+    g.vector.quantize_mx(T.qx[:, own], T.sx[:, own], T.xb[:]).then_inc(T.sem.xq, 1)
+    g.vector.wait_ge(T.sem.win, 16)
+    g.vector.quantize_mx(T.qw[:], T.sw[:], T.wb[:]).then_inc(T.sem.wq, 1)
+
+    g.wait_ge(T.sem.xq, 1)
+    sent = 0
+    for d in first[core]:
+        rid, pid = topo.addr(d, core)
+        m = topo.mask(core, d)
+        for view, sem in ((_plane, T.sem["s%d" % rank]), (_codes, T.sem["c%d" % rank])):
+            g.remote_dma(out_ap=view(T, rank), in_ap=view(T, rank), remote_sem=sem, local_sem=T.sem.sent,
+                         pid=pid, routing_id=rid, dma_engine_mask=m)
+            sent += _bits(m)
+    g.wait_ge(T.sem.sent, sent)
+
+    landed = _bits(topo.mask(core, first[core][0]))
+    order = sorted(range(N), key=lambda t: (when[core][t], t))
+
+    g.tensor.wait_ge(T.sem.wq, 1)
+    for k, t in enumerate(order):
+        if t == rank:
+            g.tensor.wait_ge(T.sem.xq, 1)
+        else:
+            g.tensor.wait_ge(T.sem["s%d" % t], landed)
+            g.tensor.wait_ge(T.sem["c%d" % t], landed)
+        if k >= BANKS:
+            g.tensor.wait_ge(T.sem.vm, k - BANKS + 1)
+        b = (k % BANKS) * BANK
+        cols = slice(t * NC, (t + 1) * NC)
+        g.tensor.matmul_mx(T.ps[:, b:b + NC], T.qw[:], T.sw[:], T.qx[:, cols], T.sx[:, cols],
+                           True, True).then_inc(T.sem["m%d" % k], 1)
+
+    for k in range(N):
+        b = (k % BANKS) * BANK
+        g.vector.wait_ge(T.sem["m%d" % k], 1)
+        if k == 0:
+            g.vector.tensor_copy(T.acc[:], T.ps[:, b:b + NC]).then_inc(T.sem.vm, 1)
+        else:
+            g.vector.wait_ge(T.sem.vm, k)
+            g.vector.tensor_tensor(T.acc[:], T.ps[:, b:b + NC], T.acc[:], AluOpType.max).then_inc(T.sem.vm, 1)
+
+    g.sync.wait_ge(T.sem.vm, N)
+    g.sync.dma_start(T.y[:], T.acc[:]).then_inc(T.sem.out, 16)
+    g.sync.wait_ge(T.sem.out, 16)

@@ -29,28 +29,33 @@ def _bits(m):
     return bin(m).count("1")
 
 
+def _lanes(m):
+    e = [b for b in range(m.bit_length()) if (m >> b) & 1]
+    return sum(1 << b for b in e[0::2]), sum(1 << b for b in e[1::2])
+
+
 def _build(T, topo):
     ranks = list(T.cores)
     hosts = sorted(set(topo.host(r) for r in ranks))
     row = {}
     for h in hosts:
         row[h] = sorted([r for r in ranks if topo.host(r) == h], key=topo.chip)
-    helpers = {}
+    role = {}
     for r in ranks:
         chip = [c for c in range(WORLD) if c != r and topo.host(c) == topo.host(r) and topo.chip(c) == topo.chip(r)]
         other = [c for c in chip if topo.die(c) != topo.die(r)]
         same = [c for c in chip if topo.die(c) == topo.die(r)]
-        helpers[r] = (other[1], other[0], same[-1], other[2])
-    first, relay = {}, {}
+        role[r] = {"F": other[1], "P1": other[0], "K": other[2], "P2": same[-1], "P3": same[0]}
+    first, relay, lands = {}, {}, {}
     when = {}
     for r in ranks:
         when[r] = {}
-    lag = 1.5
+    S, C, L, O = 1.0, 1.5, 0.6, 0.8
     for t, r in enumerate(ranks):
         h = topo.host(r)
         n = len(row[h])
         i = row[h].index(r)
-        mate_host = [k for k in hosts if k != h and topo.rack(k) == topo.rack(h)][0]
+        m = [k for k in hosts if k != h and topo.rack(k) == topo.rack(h)][0]
         far = [k for k in hosts if topo.rack(k) != topo.rack(h)]
         cabled = [k for k in far if topo.may_write(r, row[k][i])][0]
         diagonal = [k for k in far if k != cabled][0]
@@ -58,24 +63,38 @@ def _build(T, topo):
         def at(k, s):
             return row[k][(i + s) % n]
 
-        tree = [
-            (at(cabled, 0), [at(diagonal, s) for s in range(n)]),
-            (at(h, 1), [at(cabled, 1), at(mate_host, 1), at(mate_host, 0)]),
-            (at(h, 2), [at(cabled, 2), at(mate_host, 2)]),
-            (at(h, 3), [at(cabled, 3)]),
+        kcore = role[at(m, 0)]["K"]
+        jobs = [
+            ("F", at(cabled, 0), C, None, [at(diagonal, 1), at(diagonal, 2), at(diagonal, 3)]),
+            ("P1", at(h, 1), S, at(cabled, 1), [kcore, at(m, 1)]),
+            ("K", at(m, 0), 2 * S + L, at(diagonal, 0), []),
+            ("P2", at(h, 2), 2 * S, at(cabled, 2), [at(m, 2)]),
+            ("P3", at(h, 3), 3 * S, at(cabled, 3), []),
         ]
-        first[r] = []
-        for j, (home, kids) in enumerate(tree):
-            q = helpers[home][j]
-            first[r].append(q)
-            relay[q] = (t, home, kids)
-            when[home][t] = j + 1 + lag + 1
-            for k, d in enumerate(kids):
-                when[d][t] = j + 1 + lag + k + 1
-        first[r].append(at(mate_host, 3))
-        when[at(mate_host, 3)][t] = len(tree) + 1
+        for name, home, t0, cable, switch in jobs:
+            q = role[home][name]
+            relay[q] = (t, home, cable, switch)
+            away = topo.mask(q, cable if cable is not None else switch[0])
+            here = topo.mask(q, home) & ~away
+            a, b = _lanes(away) if (cable is not None and switch) else (away, away)
+            lands[(home, t)] = _bits(here)
+            when[home][t] = t0 + L + O
+            if cable is not None:
+                lands[(cable, t)] = _bits(b)
+                when[cable][t] = t0 + L + C
+            for k, d in enumerate(switch):
+                lands[(d, t)] = _bits(a)
+                if d in when:
+                    when[d][t] = t0 + L + (k + 1) * S
+        leaf = at(m, 3)
+        first[r] = (role[at(cabled, 0)]["F"], [role[at(h, 1)]["P1"], role[at(h, 2)]["P2"], role[at(h, 3)]["P3"], leaf])
+        a, b = _lanes(topo.mask(r, leaf))
+        lands[(first[r][0], t)] = _bits(b)
+        for d in first[r][1]:
+            lands[(d, t)] = _bits(a)
+        when[leaf][t] = 4 * S
         when[r][t] = 0
-    return first, relay, when
+    return first, relay, lands, when
 
 
 def _codes(T, t):
@@ -86,37 +105,46 @@ def _plane(T, t):
     return T.sx[:, t * NC:(t + 1) * NC]
 
 
-def _helper(g, core, T, topo, job):
-    t, home, kids = job
-    away = topo.mask(core, kids[0])
+def _one(topo, core, d, mask, sem, ap):
+    rid, pid = topo.addr(d, core)
+    return RemoteDMATransfer(dst_ids=[DstId(rid=rid, pnc=pid)], dma_engine_mask=mask, remote_sem=sem, src=ap, dst=ap)
+
+
+def _helper(g, core, T, topo, job, need):
+    t, home, cable, switch = job
+    away = topo.mask(core, cable if cable is not None else switch[0])
     here = topo.mask(core, home) & ~away
-    ids = []
-    for d in kids:
-        rid, pid = topo.addr(d, core)
-        ids.append(DstId(rid=rid, pnc=pid))
-    rid, pid = topo.addr(home, core)
-    home_id = DstId(rid=rid, pnc=pid)
+    a, b = _lanes(away) if (cable is not None and switch) else (away, away)
     sent = 0
     for view, sem in ((_plane, T.sem["s%d" % t]), (_codes, T.sem["c%d" % t])):
-        g.wait_ge(sem, _bits(away))
-        g.remote_dma_fused([
-            RemoteDMATransfer(dst_ids=ids, dma_engine_mask=away, remote_sem=sem,
-                              srcs=[view(T, t)], dsts=[view(T, t) for d in kids]),
-            RemoteDMATransfer(dst_ids=[home_id], dma_engine_mask=here, remote_sem=sem,
-                              src=view(T, t), dst=view(T, t)),
-        ], local_sem=T.sem.sent)
-        sent += _bits(away) + _bits(here)
+        ap = view(T, t)
+        g.wait_ge(sem, need)
+        tr = []
+        if cable is not None:
+            tr.append(_one(topo, core, cable, b, sem, ap))
+            sent += _bits(b)
+        if switch:
+            tr.append(_one(topo, core, switch[0], a, sem, ap))
+            sent += _bits(a)
+        tr.append(_one(topo, core, home, here, sem, ap))
+        sent += _bits(here)
+        g.remote_dma_fused(tr, local_sem=T.sem.sent)
+        for d in switch[1:]:
+            rid, pid = topo.addr(d, core)
+            g.remote_dma(out_ap=ap, in_ap=ap, remote_sem=sem, local_sem=T.sem.sent,
+                         pid=pid, routing_id=rid, dma_engine_mask=a)
+            sent += _bits(a)
     g.wait_ge(T.sem.sent, sent)
 
 
 def rank_program(g, core, T, topo):
     if "plan" not in _CACHE:
         _CACHE["plan"] = _build(T, topo)
-    first, relay, when = _CACHE["plan"]
+    first, relay, lands, when = _CACHE["plan"]
     rank = T.rank_of(core)
     if rank is None:
         if core in relay:
-            _helper(g, core, T, topo, relay[core])
+            _helper(g, core, T, topo, relay[core], lands[(core, relay[core][0])])
         return
 
     g.sync.dma_start(T.xb[:], T.x[:]).then_inc(T.sem.xin, 16)
@@ -129,18 +157,24 @@ def rank_program(g, core, T, topo):
     g.vector.wait_ge(T.sem.win, 16)
     g.vector.quantize_mx(T.qw[:], T.sw[:], T.wb[:]).then_inc(T.sem.wq, 1)
 
+    far, near = first[core]
+    a, b = _lanes(topo.mask(core, near[0]))
+    pairs = ((_plane, T.sem["s%d" % rank]), (_codes, T.sem["c%d" % rank]))
     g.wait_ge(T.sem.xq, 1)
     sent = 0
-    for d in first[core]:
+    for view, sem in pairs:
+        ap = view(T, rank)
+        g.remote_dma_fused([_one(topo, core, far, b, sem, ap), _one(topo, core, near[0], a, sem, ap)],
+                           local_sem=T.sem.sent)
+        sent += _bits(a) + _bits(b)
+    for d in near[1:]:
         rid, pid = topo.addr(d, core)
-        m = topo.mask(core, d)
-        for view, sem in ((_plane, T.sem["s%d" % rank]), (_codes, T.sem["c%d" % rank])):
+        for view, sem in pairs:
             g.remote_dma(out_ap=view(T, rank), in_ap=view(T, rank), remote_sem=sem, local_sem=T.sem.sent,
-                         pid=pid, routing_id=rid, dma_engine_mask=m)
-            sent += _bits(m)
+                         pid=pid, routing_id=rid, dma_engine_mask=a)
+            sent += _bits(a)
     g.wait_ge(T.sem.sent, sent)
 
-    landed = _bits(topo.mask(core, first[core][0]))
     order = sorted(range(N), key=lambda t: (when[core][t], t))
 
     g.tensor.wait_ge(T.sem.wq, 1)
@@ -148,23 +182,23 @@ def rank_program(g, core, T, topo):
         if t == rank:
             g.tensor.wait_ge(T.sem.xq, 1)
         else:
-            g.tensor.wait_ge(T.sem["s%d" % t], landed)
-            g.tensor.wait_ge(T.sem["c%d" % t], landed)
+            g.tensor.wait_ge(T.sem["s%d" % t], lands[(core, t)])
+            g.tensor.wait_ge(T.sem["c%d" % t], lands[(core, t)])
         if k >= BANKS:
             g.tensor.wait_ge(T.sem.vm, k - BANKS + 1)
-        b = (k % BANKS) * BANK
+        b0 = (k % BANKS) * BANK
         cols = slice(t * NC, (t + 1) * NC)
-        g.tensor.matmul_mx(T.ps[:, b:b + NC], T.qw[:], T.sw[:], T.qx[:, cols], T.sx[:, cols],
+        g.tensor.matmul_mx(T.ps[:, b0:b0 + NC], T.qw[:], T.sw[:], T.qx[:, cols], T.sx[:, cols],
                            True, True).then_inc(T.sem["m%d" % k], 1)
 
     for k in range(N):
-        b = (k % BANKS) * BANK
+        b0 = (k % BANKS) * BANK
         g.vector.wait_ge(T.sem["m%d" % k], 1)
         if k == 0:
-            g.vector.tensor_copy(T.acc[:], T.ps[:, b:b + NC]).then_inc(T.sem.vm, 1)
+            g.vector.tensor_copy(T.acc[:], T.ps[:, b0:b0 + NC]).then_inc(T.sem.vm, 1)
         else:
             g.vector.wait_ge(T.sem.vm, k)
-            g.vector.tensor_tensor(T.acc[:], T.ps[:, b:b + NC], T.acc[:], AluOpType.max).then_inc(T.sem.vm, 1)
+            g.vector.tensor_tensor(T.acc[:], T.ps[:, b0:b0 + NC], T.acc[:], AluOpType.max).then_inc(T.sem.vm, 1)
 
     g.sync.wait_ge(T.sem.vm, N)
     g.sync.dma_start(T.y[:], T.acc[:]).then_inc(T.sem.out, 16)

from concourse.bass import DstId, RemoteDMATransfer
from concourse.mybir import dt, AluOpType

N = 16
NC = 256
WORLD = 512
BANK = 512
BANKS = 8

SCRATCH = {
    "xb": ("sbuf", [128, 4 * NC], "bfloat16"),
    "wb": ("sbuf", [128, 512], "bfloat16"),
    "qw": ("sbuf", [128, 128], "float8_e4m3fn_x4"),
    "sw": ("sbuf", [128, 128], "uint8"),
    "qx": ("sbuf", [128, N * NC], "float8_e4m3fn_x4"),
    "sx": ("sbuf", [128, N * NC], "uint8"),
    "acc": ("sbuf", [128, NC], "float32"),
    "ps": ("psum", [128, BANK * BANKS], "float32"),
}
SEMAPHORES = (["xin", "win", "xq", "wq", "vm", "out", "sent"]
              + ["c%d" % t for t in range(N)]
              + ["s%d" % t for t in range(N)]
              + ["m%d" % t for t in range(N)])

_CACHE = {}


def _bits(m):
    return bin(m).count("1")


def _lanes(m):
    e = [b for b in range(m.bit_length()) if (m >> b) & 1]
    return sum(1 << b for b in e[0::2]), sum(1 << b for b in e[1::2])


def _build(T, topo):
    ranks = list(T.cores)
    hosts = sorted(set(topo.host(r) for r in ranks))
    row = {}
    for h in hosts:
        row[h] = sorted([r for r in ranks if topo.host(r) == h], key=topo.chip)
    role = {}
    for r in ranks:
        chip = [c for c in range(WORLD) if c != r and topo.host(c) == topo.host(r) and topo.chip(c) == topo.chip(r)]
        other = [c for c in chip if topo.die(c) != topo.die(r)]
        same = [c for c in chip if topo.die(c) == topo.die(r)]
        role[r] = {"F": other[1], "P1": other[0], "K": other[2], "P2": same[-1], "P3": same[0]}
    first, relay, lands = {}, {}, {}
    when = {}
    for r in ranks:
        when[r] = {}
    S, C, L, O = 1.0, 1.5, 0.6, 0.8
    for t, r in enumerate(ranks):
        h = topo.host(r)
        n = len(row[h])
        i = row[h].index(r)
        m = [k for k in hosts if k != h and topo.rack(k) == topo.rack(h)][0]
        far = [k for k in hosts if topo.rack(k) != topo.rack(h)]
        cabled = [k for k in far if topo.may_write(r, row[k][i])][0]
        diagonal = [k for k in far if k != cabled][0]

        def at(k, s):
            return row[k][(i + s) % n]

        kcore = role[at(m, 0)]["K"]
        jobs = [
            ("F", at(cabled, 0), C, None, [at(diagonal, 1), at(diagonal, 2), at(diagonal, 3)]),
            ("P1", at(h, 1), S, at(cabled, 1), [kcore, at(m, 1)]),
            ("K", at(m, 0), 2 * S + L, at(diagonal, 0), []),
            ("P2", at(h, 2), 2 * S, at(cabled, 2), [at(m, 2)]),
            ("P3", at(h, 3), 3 * S, at(cabled, 3), []),
        ]
        for name, home, t0, cable, switch in jobs:
            q = role[home][name]
            relay[q] = (t, home, cable, switch)
            away = topo.mask(q, cable if cable is not None else switch[0])
            here = topo.mask(q, home) & ~away
            a, b = _lanes(away) if (cable is not None and switch) else (away, away)
            lands[(home, t)] = _bits(here)
            when[home][t] = t0 + L + O
            if cable is not None:
                lands[(cable, t)] = _bits(b)
                when[cable][t] = t0 + L + C
            for k, d in enumerate(switch):
                lands[(d, t)] = _bits(a)
                if d in when:
                    when[d][t] = t0 + L + (k + 1) * S
        leaf = at(m, 3)
        first[r] = (role[at(cabled, 0)]["F"], [role[at(h, 1)]["P1"], role[at(h, 2)]["P2"], role[at(h, 3)]["P3"], leaf])
        a, b = _lanes(topo.mask(r, leaf))
        lands[(first[r][0], t)] = _bits(b)
        for d in first[r][1]:
            lands[(d, t)] = _bits(a)
        when[leaf][t] = 4 * S
        when[r][t] = 0
    return first, relay, lands, when


def _codes(T, t):
    return T.qx[:, t * NC:(t + 1) * NC].bitcast(dt.uint8)


def _plane(T, t):
    return T.sx[:, t * NC:(t + 1) * NC]


def _one(topo, core, d, mask, sem, ap):
    rid, pid = topo.addr(d, core)
    return RemoteDMATransfer(dst_ids=[DstId(rid=rid, pnc=pid)], dma_engine_mask=mask, remote_sem=sem, src=ap, dst=ap)


def _helper(g, core, T, topo, job, need):
    t, home, cable, switch = job
    away = topo.mask(core, cable if cable is not None else switch[0])
    here = topo.mask(core, home) & ~away
    a, b = _lanes(away) if (cable is not None and switch) else (away, away)
    sent = 0
    for view, sem in ((_plane, T.sem["s%d" % t]), (_codes, T.sem["c%d" % t])):
        ap = view(T, t)
        g.wait_ge(sem, need)
        tr = []
        if cable is not None:
            tr.append(_one(topo, core, cable, b, sem, ap))
            sent += _bits(b)
        if switch:
            tr.append(_one(topo, core, switch[0], a, sem, ap))
            sent += _bits(a)
        tr.append(_one(topo, core, home, here, sem, ap))
        sent += _bits(here)
        g.remote_dma_fused(tr, local_sem=T.sem.sent)
        for d in switch[1:]:
            rid, pid = topo.addr(d, core)
            g.remote_dma(out_ap=ap, in_ap=ap, remote_sem=sem, local_sem=T.sem.sent,
                         pid=pid, routing_id=rid, dma_engine_mask=a)
            sent += _bits(a)
    g.wait_ge(T.sem.sent, sent)


def rank_program(g, core, T, topo):
    if "plan" not in _CACHE:
        _CACHE["plan"] = _build(T, topo)
    first, relay, lands, when = _CACHE["plan"]
    rank = T.rank_of(core)
    if rank is None:
        if core in relay:
            _helper(g, core, T, topo, relay[core], lands[(core, relay[core][0])])
        return

    g.sync.dma_start(T.xb[:], T.x[:]).then_inc(T.sem.xin, 16)
    g.scalar.wait_ge(T.sem.xin, 16)
    g.scalar.dma_start(T.wb[:], T.w[:]).then_inc(T.sem.win, 16)

    own = slice(rank * NC, (rank + 1) * NC)
    g.vector.wait_ge(T.sem.xin, 16)
    g.vector.quantize_mx(T.qx[:, own], T.sx[:, own], T.xb[:]).then_inc(T.sem.xq, 1)
    g.vector.wait_ge(T.sem.win, 16)
    g.vector.quantize_mx(T.qw[:], T.sw[:], T.wb[:]).then_inc(T.sem.wq, 1)

    far, near = first[core]
    a, b = _lanes(topo.mask(core, near[0]))
    pairs = ((_plane, T.sem["s%d" % rank]), (_codes, T.sem["c%d" % rank]))
    g.wait_ge(T.sem.xq, 1)
    sent = 0
    for view, sem in pairs:
        ap = view(T, rank)
        g.remote_dma_fused([_one(topo, core, far, b, sem, ap), _one(topo, core, near[0], a, sem, ap)],
                           local_sem=T.sem.sent)
        sent += _bits(a) + _bits(b)
    for d in near[1:]:
        rid, pid = topo.addr(d, core)
        for view, sem in pairs:
            g.remote_dma(out_ap=view(T, rank), in_ap=view(T, rank), remote_sem=sem, local_sem=T.sem.sent,
                         pid=pid, routing_id=rid, dma_engine_mask=a)
            sent += _bits(a)
    g.wait_ge(T.sem.sent, sent)

    order = sorted(range(N), key=lambda t: (when[core][t], t))

    g.tensor.wait_ge(T.sem.wq, 1)
    for k, t in enumerate(order):
        if t == rank:
            g.tensor.wait_ge(T.sem.xq, 1)
        else:
            g.tensor.wait_ge(T.sem["s%d" % t], lands[(core, t)])
            g.tensor.wait_ge(T.sem["c%d" % t], lands[(core, t)])
        if k >= BANKS:
            g.tensor.wait_ge(T.sem.vm, k - BANKS + 1)
        b0 = (k % BANKS) * BANK
        cols = slice(t * NC, (t + 1) * NC)
        g.tensor.matmul_mx(T.ps[:, b0:b0 + NC], T.qw[:], T.sw[:], T.qx[:, cols], T.sx[:, cols],
                           True, True).then_inc(T.sem["m%d" % k], 1)

    for k in range(N):
        b0 = (k % BANKS) * BANK
        g.vector.wait_ge(T.sem["m%d" % k], 1)
        if k == 0:
            g.vector.tensor_copy(T.acc[:], T.ps[:, b0:b0 + NC]).then_inc(T.sem.vm, 1)
        else:
            g.vector.wait_ge(T.sem.vm, k)
            g.vector.tensor_tensor(T.acc[:], T.ps[:, b0:b0 + NC], T.acc[:], AluOpType.max).then_inc(T.sem.vm, 1)

    g.sync.wait_ge(T.sem.vm, N)
    g.sync.dma_start(T.y[:], T.acc[:]).then_inc(T.sem.out, 16)
    g.sync.wait_ge(T.sem.out, 16)
